import numpy as np, ml_dtypes
CORES = [10,34,74,98]
N = 4
import mx_ref
BF = ml_dtypes.bfloat16
def rowtile(v, k):
    z = np.concatenate([v, np.zeros((1, v.shape[1]), BF)])
    return np.concatenate([np.ascontiguousarray(z[k[:, 4 * m:4 * m + 4]].transpose(0, 2, 1)).reshape(128, -1) for m in range(k.shape[1] // 4)], axis=1)
def cut(t, i, w=512):
    return t[:, w * i:w * i + w]
def f(rng, *shape):
    return mx_ref.flush((rng.standard_normal(shape, dtype=np.float32) * np.exp2(rng.integers(-2, 3, shape[:-1] + (1,)))).astype(BF))
def wide(rng, *shape, cols=0):
    v = rng.standard_normal(shape, dtype=np.float32) * np.exp2(rng.integers(-12, 13, shape)).astype(np.float32)
    if cols: v *= np.repeat(np.exp2(rng.integers(-cols, cols + 1, shape[:-2] + (1, shape[-1] // 4))) * (rng.random(shape[:-2] + (1, shape[-1] // 4)) > 0.0625), 4, axis=-1).astype(np.float32)
    return mx_ref.flush(v.astype(BF))
T, GW, CAPP = 1024, 512, 256
def counts(rng):
    n = rng.integers(0, CAPP + 1, (N, N))
    for e in range(N):
        if n[:, e].sum() < CAPP: n[rng.integers(0, N), e] = CAPP
    return n
def lists(rng, n):
    l = np.full((N, N, 512), -1)
    for s in range(N):
        for e in range(N): l[s, e, :n[s, e]] = rng.integers(0, T, n[s, e])
    return l
def store(l):
    return np.ascontiguousarray(l.reshape(N, N, 128, 4).transpose(0, 2, 1, 3)).reshape(N, 128, 4 * N).astype(np.int32)
def setup_inputs(rng):
    return {"x": f(rng, N, T, 128), "dy": f(rng, N, T, GW), "pick": store(lists(rng, counts(rng)))}
def setup_inputs_alike(rng):
    d = setup_inputs(rng); l = np.full((N, N, 512), -1); n = rng.integers(CAPP // 2, CAPP + 1)
    l[:, :, :n] = rng.integers(0, T, n)
    d["pick"] = store(l); return d
def setup_inputs_counts(rng):
    d = setup_inputs(rng)
    n = np.array([0, 1, 33, CAPP])[(np.arange(N)[:, None] + np.arange(N) + rng.integers(0, 4)) % 4][rng.permutation(N)]
    d["pick"] = store(lists(rng, n)); return d
def setup_inputs_giant(rng):
    d = setup_inputs(rng); l = lists(rng, rng.integers(64, CAPP + 1, (N, N)))
    for s in range(N):
        k = rng.permutation(T); kx, kg = k[:T // 32], k[T // 32:T // 16]
        d["x"][s, kx] = (d["x"][s, kx].astype(np.float32) * np.float32(4096)).astype(BF)
        d["dy"][s, kg] = (d["dy"][s, kg].astype(np.float32) * np.float32(4096)).astype(BF)
        for e in range(N):
            i = rng.permutation(32)
            l[s, e, i[0]], l[s, e, i[1]] = rng.choice(kx), rng.choice(kg)
    d["pick"] = store(l); return d
def setup_inputs_reversed(rng):
    d = setup_inputs(rng); n = counts(rng); l = lists(rng, n)
    for s in range(N):
        for e in range(N): l[s, e, :n[s, e]] = np.sort(l[s, e, :n[s, e]])[::-1]
    d["pick"] = store(l); return d
def setup_inputs_spread(rng):
    d = setup_inputs(rng); d["x"] = wide(rng, N, T, 128); d["dy"] = wide(rng, N, T, GW)
    d["pick"] = store(lists(rng, rng.integers(CAPP // 2, CAPP + 1, (N, N)))); return d
def check_inputs(d):
    b = []
    for q in ("x", "dy"):
        v = np.abs(np.asarray(d[q]).astype(np.float32))
        if not np.isfinite(v).all() or ((v != 0) & ((v < 2.0 ** -30) | (v > 2.0 ** 30))).any(): b.append(q)
    for s in range(N):
        for e in range(N):
            k = np.asarray(d["pick"][s])[:, 4 * e:4 * e + 4].reshape(-1); n = int((k >= 0).sum())
            if n > CAPP or k.max() >= T or (k[:n] < 0).any() or (k[n:] != -1).any(): b.append("pick")
    return b
def reference(x, dy, pick):
    y = np.zeros((N, 128, GW), np.float32)
    for e in range(N):
        for s in range(N):
            k = pick[s][:, 4 * e:4 * e + 4]
            X, G = mx_ref.quantize(rowtile(x[s], k)), rowtile(dy[s], k)
            for i in range(GW // 512): y[e][:, 512 * i:512 * i + 512] += mx_ref.matmul(X, mx_ref.quantize(cut(G, i, 2048)))
    return {"y": y}

@@ -1,0 +1,168 @@
+from concourse.bass import DstId, RemoteDMATransfer, IndirectOffsetOnAxis
+from concourse.mybir import dt, ActivationFunctionType
+
+N = 4
+ROWS = 1024
+XW, GW = 128, 512
+RW = XW + GW
+C = 512
+HALF = GW // 2
+
+SCRATCH = {
+    "idx": ("sbuf", [128, 16], "int32"),
+    "tab": ("dram", [ROWS, RW], "bfloat16"),
+    "ps": ("psum", [128, 1024], "float32"),
+    "yo0": ("sbuf", [128, HALF], "float32"),
+    "yo1": ("sbuf", [128, HALF], "float32"),
+}
+for _k in range(N):
+    SCRATCH["land%d" % _k] = ("sbuf", [128, 2 * RW], "bfloat16")
+    SCRATCH["tile%d" % _k] = ("sbuf", [128, 4 * C], "bfloat16")
+    SCRATCH["cq%d" % _k] = ("sbuf", [128, C], "float8_e4m3fn_x4")
+    SCRATCH["sq%d" % _k] = ("sbuf", [128, C], "uint8")
+for _k in range(N - 1):
+    SCRATCH["cin%d" % _k] = ("sbuf", [128, C], "float8_e4m3fn_x4")
+    SCRATCH["sin%d" % _k] = ("sbuf", [128, C], "uint8")
+
+SEMAPHORES = ["idx", "tab", "sent", "mm0", "mm1", "yc0", "yc1", "st0", "st1"]
+for _k in range(N):
+    SEMAPHORES += ["zl%d" % _k, "zt%d" % _k, "cp%d" % _k, "qq%d" % _k, "ga%d_0" % _k, "ga%d_1" % _k]
+for _k in range(N - 1):
+    SEMAPHORES += ["arr%d" % _k]
+
+
+def rank_program(g, core, T, topo):
+    r = T.rank_of(core)
+    if r is None:
+        return
+    cores = T.cores
+    S = T.sem
+    plane = lambda m: sum(1 for a in range(N) if topo.same_plane(topo.chip(cores[a]), topo.chip(cores[a ^ m])))
+    order = sorted(range(1, N), key=lambda m: (plane(m), m))
+    lists = [r ^ m for m in order] + [r]
+    upper, lower = slice(0, 64), slice(64, 128)
+
+    g.sync.dma_start(T.idx[0:64, :], T.pick[0:64, :]).then_inc(S["idx"], 16)
+    g.scalar.dma_start(T.idx[64:128, 0:14], T.pick[0:64, 2:16]).then_inc(S["idx"], 16)
+    g.sync.dma_start(T.tab[:, XW:RW], T.dy[:]).then_inc(S["tab"], 16)
+    g.scalar.dma_start(T.tab[:, 0:XW], T.x[:]).then_inc(S["tab"], 16)
+
+    for k in range(N):
+        g.vector.memset(T["land%d" % k][:], 0.0).then_inc(S["zl%d" % k], 1)
+    for k in range(N):
+        t = T["tile%d" % k]
+        g.vector.memset(t[lower, 0:4 * XW], 0.0).then_inc(S["zt%d" % k], 1)
+        g.vector.memset(t[upper, 4 * (C - XW):4 * C], 0.0).then_inc(S["zt%d" % k], 1)
+
+    def gather(k, i, table):
+        col = 4 * lists[k] + i
+        off = IndirectOffsetOnAxis(ap=T.idx[:, col:col + 1], axis=0)
+        land, sem = T["land%d" % k], S["ga%d_%d" % (k, i)]
+        o = RW * i
+        if table:
+            g.indirect_dma_start(land[:, o:o + RW], None, T.tab[:], off, bounds_check=ROWS - 1, oob_is_err=False).then_inc(sem, 16)
+        else:
+            g.indirect_dma_start(land[:, o + XW:o + RW], None, T.dy[:], off, bounds_check=ROWS - 1, oob_is_err=False).then_inc(sem, 16)
+            g.indirect_dma_start(land[:, o:o + XW], None, T.x[:], off, bounds_check=ROWS - 1, oob_is_err=False).then_inc(sem, 16)
+
+    sent = [0]
+
+    def dest(k):
+        d = cores[lists[k]]
+        rid, pid, _ = topo.addr(d)
+        return d, rid, pid
+
+    def send_fused(k):
+        d, rid, pid = dest(k)
+        es = topo.engines(core, d)
+        per = len(es) // 4
+        groups = [es[per * a:per * (a + 1)] for a in range(4)]
+        last = groups.pop()
+        groups += [last[:per // 2], last[per // 2:]]
+        cq, cin, w = T["cq%d" % k], T["cin%d" % k], C // 4
+        tr = []
+        for a in range(5):
+            if a < 4:
+                src, dst = cq[:, w * a:w * (a + 1)].bitcast(dt.uint8), cin[:, w * a:w * (a + 1)].bitcast(dt.uint8)
+            else:
+                src, dst = T["sq%d" % k][:], T["sin%d" % k][:]
+            tr.append(RemoteDMATransfer(dst_ids=[DstId(rid=rid, pnc=pid)], dma_engine_mask=sum(1 << e for e in groups[a]),
+                                        remote_sem=S["arr%d" % k], src=src, dst=dst))
+        g.remote_dma_fused(tr, local_sem=S["sent"])
+        sent[0] += len(es)
+
+    def send_split(k):
+        d, rid, pid = dest(k)
+        m, n = topo.mask(core, d), len(topo.engines(core, d))
+        g.remote_dma(T["cin%d" % k][:].bitcast(dt.uint8), T["cq%d" % k][:].bitcast(dt.uint8),
+                     S["arr%d" % k], S["sent"], pid, rid, m)
+        g.remote_dma(T["sin%d" % k][:], T["sq%d" % k][:], S["arr%d" % k], S["sent"], pid, rid, m)
+        sent[0] += 2 * n
+
+    def arrivals(k):
+        n = len(topo.engines(cores[lists[k]], core))
+        return n if k < 2 else 2 * n
+
+    g.wait_ge(S["idx"], 32)
+    g.wait_ge(S["zl0"], 1)
+    gather(0, 0, False)
+    gather(0, 1, False)
+    g.wait_ge(S["tab"], 32)
+    g.wait_ge(S["zl1"], 1)
+    gather(1, 0, True)
+    gather(1, 1, True)
+    g.wait_ge(S["qq0"], 1)
+    send_fused(0)
+    g.wait_ge(S["zl2"], 1)
+    gather(2, 0, True)
+    gather(2, 1, True)
+    g.wait_ge(S["qq1"], 1)
+    send_fused(1)
+    g.wait_ge(S["zl3"], 1)
+    gather(3, 0, True)
+    gather(3, 1, True)
+    g.wait_ge(S["qq2"], 1)
+    send_split(2)
+    g.wait_ge(S["sent"], sent[0])
+
+    for k in range(N):
+        land, tile, cp = T["land%d" % k], T["tile%d" % k], S["cp%d" % k]
+        for i in range(2):
+            n = 32 if k == 0 else 16
+            g.vector.wait_ge(S["ga%d_%d" % (k, i)], n)
+            g.scalar.wait_ge(S["ga%d_%d" % (k, i)], n)
+            o = RW * i
+            for s, p in ((0, upper), (1, lower)):
+                t = i + 2 * s
+                g.vector.tensor_copy(tile[upper, t:4 * (XW + HALF):4], land[p, o:o + XW + HALF]).then_inc(cp, 1)
+                parts = ((tile[lower, 4 * XW + t:4 * (XW + HALF):4], land[p, o + XW + HALF:o + RW]),
+                         (tile[lower, 4 * (XW + HALF) + t:4 * C:4], land[p, o:o + XW]))
+                for a, b in parts:
+                    if s == 0:
+                        g.vector.tensor_copy(a, b).then_inc(cp, 1)
+                    else:
+                        g.scalar.activation(a, b, ActivationFunctionType.Copy).then_inc(cp, 1)
+        g.vector.wait_ge(S["zt%d" % k], 2)
+        g.vector.wait_ge(cp, 12)
+        g.vector.quantize_mx(T["cq%d" % k][:], T["sq%d" % k][:], tile[:]).then_inc(S["qq%d" % k], 1)
+
+    steps = [("cin0", "sin0", "arr0", arrivals(0)), ("cin1", "sin1", "arr1", arrivals(1)), ("cq3", "sq3", "qq3", 1),
+             ("cin2", "sin2", "arr2", arrivals(2))]
+    for j, (c, s, sem, n) in enumerate(steps):
+        g.tensor.wait_ge(S[sem], n)
+        for h, a in ((0, 0), (1, C - XW)):
+            op = g.tensor.matmul_mx(T.ps[:, 512 * h:512 * h + HALF], T[c][:, a:a + XW], T[s][:, a:a + XW],
+                                    T[c][:, XW:XW + HALF], T[s][:, XW:XW + HALF], j == 0, j == len(steps) - 1)
+            if j == len(steps) - 1:
+                op.then_inc(S["mm%d" % h], 1)
+
+    g.vector.wait_ge(S["mm0"], 1)
+    g.vector.tensor_copy(T.yo0[:], T.ps[:, 0:HALF]).then_inc(S["yc0"], 1)
+    g.sync.wait_ge(S["yc0"], 1)
+    g.sync.dma_start(T.y[:, 0:HALF], T.yo0[:]).then_inc(S["st0"], 16)
+    g.sync.wait_ge(S["st0"], 16)
+    g.scalar.wait_ge(S["mm1"], 1)
+    g.scalar.activation(T.yo1[:], T.ps[:, 512:512 + HALF], ActivationFunctionType.Copy).then_inc(S["yc1"], 1)
+    g.scalar.wait_ge(S["yc1"], 1)
+    g.scalar.dma_start(T.y[:, HALF:GW], T.yo1[:]).then_inc(S["st1"], 16)
+    g.scalar.wait_ge(S["st1"], 16)

@@ -1,6 +1,8 @@
 from concourse.bass import DstId, RemoteDMATransfer, IndirectOffsetOnAxis
 from concourse.mybir import dt, ActivationFunctionType
 
+PLAN = "d00 tab t01 t10 t11 f0 t20 t21 f1 t30 t31 s2".split()
+
 N = 4
 ROWS = 1024
 XW, GW = 128, 512
@@ -24,7 +26,7 @@ for _k in range(N - 1):
     SCRATCH["cin%d" % _k] = ("sbuf", [128, C], "float8_e4m3fn_x4")
     SCRATCH["sin%d" % _k] = ("sbuf", [128, C], "uint8")
 
-SEMAPHORES = ["idx", "tab", "sent", "mm0", "mm1", "yc0", "yc1", "st0", "st1"]
+SEMAPHORES = ["idx", "tab", "tabx", "sent", "mm0", "mm1", "yc0", "yc1", "st0", "st1"]
 for _k in range(N):
     SEMAPHORES += ["zl%d" % _k, "zt%d" % _k, "cp%d" % _k, "qq%d" % _k, "ga%d_0" % _k, "ga%d_1" % _k]
 for _k in range(N - 1):
@@ -45,7 +47,7 @@ def rank_program(g, core, T, topo):
     g.sync.dma_start(T.idx[0:64, :], T.pick[0:64, :]).then_inc(S["idx"], 16)
     g.scalar.dma_start(T.idx[64:128, 0:14], T.pick[0:64, 2:16]).then_inc(S["idx"], 16)
     g.sync.dma_start(T.tab[:, XW:RW], T.dy[:]).then_inc(S["tab"], 16)
-    g.scalar.dma_start(T.tab[:, 0:XW], T.x[:]).then_inc(S["tab"], 16)
+    g.dma_start(T.tab[:, 0:XW], T.x[:]).then_inc(S["tabx"], 16)
 
     for k in range(N):
         g.vector.memset(T["land%d" % k][:], 0.0).then_inc(S["zl%d" % k], 1)
@@ -101,34 +103,27 @@ def rank_program(g, core, T, topo):
 
     def arrivals(k):
         n = len(topo.engines(cores[lists[k]], core))
-        return n if k < 2 else 2 * n
+        return n if "f%d" % k in PLAN else 2 * n
 
     g.wait_ge(S["idx"], 32)
-    g.wait_ge(S["zl0"], 1)
-    gather(0, 0, False)
-    gather(0, 1, False)
-    g.wait_ge(S["tab"], 32)
-    g.wait_ge(S["zl1"], 1)
-    gather(1, 0, True)
-    gather(1, 1, True)
-    g.wait_ge(S["qq0"], 1)
-    send_fused(0)
-    g.wait_ge(S["zl2"], 1)
-    gather(2, 0, True)
-    gather(2, 1, True)
-    g.wait_ge(S["qq1"], 1)
-    send_fused(1)
-    g.wait_ge(S["zl3"], 1)
-    gather(3, 0, True)
-    gather(3, 1, True)
-    g.wait_ge(S["qq2"], 1)
-    send_split(2)
+    for step in PLAN:
+        op, k = step[0], int(step[1]) if step != "tab" else 0
+        if step == "tab":
+            g.wait_ge(S["tabx"], 16)
+            g.wait_ge(S["tab"], 16)
+        elif op in "dt":
+            if step[2] == "0":
+                g.wait_ge(S["zl%d" % k], 1)
+            gather(k, int(step[2]), op == "t")
+        else:
+            g.wait_ge(S["qq%d" % k], 1)
+            send_fused(k) if op == "f" else send_split(k)
     g.wait_ge(S["sent"], sent[0])
 
     for k in range(N):
         land, tile, cp = T["land%d" % k], T["tile%d" % k], S["cp%d" % k]
         for i in range(2):
-            n = 32 if k == 0 else 16
+            n = 32 if "d%d%d" % (k, i) in PLAN else 16
             g.vector.wait_ge(S["ga%d_%d" % (k, i)], n)
             g.scalar.wait_ge(S["ga%d_%d" % (k, i)], n)
             o = RW * i

from concourse.bass import DstId, RemoteDMATransfer, IndirectOffsetOnAxis
from concourse.mybir import dt, ActivationFunctionType

PLAN = "d00 tab t01 t10 t11 f0 t20 t21 f1 t30 t31 s2".split()

N = 4
ROWS = 1024
XW, GW = 128, 512
RW = XW + GW
C = 512
HALF = GW // 2

SCRATCH = {
    "idx": ("sbuf", [128, 16], "int32"),
    "tab": ("dram", [ROWS, RW], "bfloat16"),
    "ps": ("psum", [128, 1024], "float32"),
    "yo0": ("sbuf", [128, HALF], "float32"),
    "yo1": ("sbuf", [128, HALF], "float32"),
}
for _k in range(N):
    SCRATCH["land%d" % _k] = ("sbuf", [128, 2 * RW], "bfloat16")
    SCRATCH["tile%d" % _k] = ("sbuf", [128, 4 * C], "bfloat16")
    SCRATCH["cq%d" % _k] = ("sbuf", [128, C], "float8_e4m3fn_x4")
    SCRATCH["sq%d" % _k] = ("sbuf", [128, C], "uint8")
for _k in range(N - 1):
    SCRATCH["cin%d" % _k] = ("sbuf", [128, C], "float8_e4m3fn_x4")
    SCRATCH["sin%d" % _k] = ("sbuf", [128, C], "uint8")

SEMAPHORES = ["idx", "tab", "tabx", "sent", "mm0", "mm1", "yc0", "yc1", "st0", "st1"]
for _k in range(N):
    SEMAPHORES += ["zl%d" % _k, "zt%d" % _k, "cp%d" % _k, "qq%d" % _k, "ga%d_0" % _k, "ga%d_1" % _k]
for _k in range(N - 1):
    SEMAPHORES += ["arr%d" % _k]


def rank_program(g, core, T, topo):
    r = T.rank_of(core)
    if r is None:
        return
    cores = T.cores
    S = T.sem
    plane = lambda m: sum(1 for a in range(N) if topo.same_plane(topo.chip(cores[a]), topo.chip(cores[a ^ m])))
    order = sorted(range(1, N), key=lambda m: (plane(m), m))
    lists = [r ^ m for m in order] + [r]
    upper, lower = slice(0, 64), slice(64, 128)

    g.sync.dma_start(T.idx[0:64, :], T.pick[0:64, :]).then_inc(S["idx"], 16)
    g.scalar.dma_start(T.idx[64:128, 0:14], T.pick[0:64, 2:16]).then_inc(S["idx"], 16)
    g.sync.dma_start(T.tab[:, XW:RW], T.dy[:]).then_inc(S["tab"], 16)
    g.dma_start(T.tab[:, 0:XW], T.x[:]).then_inc(S["tabx"], 16)

    for k in range(N):
        g.vector.memset(T["land%d" % k][:], 0.0).then_inc(S["zl%d" % k], 1)
    for k in range(N):
        t = T["tile%d" % k]
        g.vector.memset(t[lower, 0:4 * XW], 0.0).then_inc(S["zt%d" % k], 1)
        g.vector.memset(t[upper, 4 * (C - XW):4 * C], 0.0).then_inc(S["zt%d" % k], 1)

    def gather(k, i, table):
        col = 4 * lists[k] + i
        off = IndirectOffsetOnAxis(ap=T.idx[:, col:col + 1], axis=0)
        land, sem = T["land%d" % k], S["ga%d_%d" % (k, i)]
        o = RW * i
        if table:
            g.indirect_dma_start(land[:, o:o + RW], None, T.tab[:], off, bounds_check=ROWS - 1, oob_is_err=False).then_inc(sem, 16)
        else:
            g.indirect_dma_start(land[:, o + XW:o + RW], None, T.dy[:], off, bounds_check=ROWS - 1, oob_is_err=False).then_inc(sem, 16)
            g.indirect_dma_start(land[:, o:o + XW], None, T.x[:], off, bounds_check=ROWS - 1, oob_is_err=False).then_inc(sem, 16)

    sent = [0]

    def dest(k):
        d = cores[lists[k]]
        rid, pid, _ = topo.addr(d)
        return d, rid, pid

    def send_fused(k):
        d, rid, pid = dest(k)
        es = topo.engines(core, d)
        per = len(es) // 4
        groups = [es[per * a:per * (a + 1)] for a in range(4)]
        last = groups.pop()
        groups += [last[:per // 2], last[per // 2:]]
        cq, cin, w = T["cq%d" % k], T["cin%d" % k], C // 4
        tr = []
        for a in range(5):
            if a < 4:
                src, dst = cq[:, w * a:w * (a + 1)].bitcast(dt.uint8), cin[:, w * a:w * (a + 1)].bitcast(dt.uint8)
            else:
                src, dst = T["sq%d" % k][:], T["sin%d" % k][:]
            tr.append(RemoteDMATransfer(dst_ids=[DstId(rid=rid, pnc=pid)], dma_engine_mask=sum(1 << e for e in groups[a]),
                                        remote_sem=S["arr%d" % k], src=src, dst=dst))
        g.remote_dma_fused(tr, local_sem=S["sent"])
        sent[0] += len(es)

    def send_split(k):
        d, rid, pid = dest(k)
        m, n = topo.mask(core, d), len(topo.engines(core, d))
        g.remote_dma(T["cin%d" % k][:].bitcast(dt.uint8), T["cq%d" % k][:].bitcast(dt.uint8),
                     S["arr%d" % k], S["sent"], pid, rid, m)
        g.remote_dma(T["sin%d" % k][:], T["sq%d" % k][:], S["arr%d" % k], S["sent"], pid, rid, m)
        sent[0] += 2 * n

    def arrivals(k):
        n = len(topo.engines(cores[lists[k]], core))
        return n if "f%d" % k in PLAN else 2 * n

    g.wait_ge(S["idx"], 32)
    for step in PLAN:
        op, k = step[0], int(step[1]) if step != "tab" else 0
        if step == "tab":
            g.wait_ge(S["tabx"], 16)
            g.wait_ge(S["tab"], 16)
        elif op in "dt":
            if step[2] == "0":
                g.wait_ge(S["zl%d" % k], 1)
            gather(k, int(step[2]), op == "t")
        else:
            g.wait_ge(S["qq%d" % k], 1)
            send_fused(k) if op == "f" else send_split(k)
    g.wait_ge(S["sent"], sent[0])

    for k in range(N):
        land, tile, cp = T["land%d" % k], T["tile%d" % k], S["cp%d" % k]
        for i in range(2):
            n = 32 if "d%d%d" % (k, i) in PLAN else 16
            g.vector.wait_ge(S["ga%d_%d" % (k, i)], n)
            g.scalar.wait_ge(S["ga%d_%d" % (k, i)], n)
            o = RW * i
            for s, p in ((0, upper), (1, lower)):
                t = i + 2 * s
                g.vector.tensor_copy(tile[upper, t:4 * (XW + HALF):4], land[p, o:o + XW + HALF]).then_inc(cp, 1)
                parts = ((tile[lower, 4 * XW + t:4 * (XW + HALF):4], land[p, o + XW + HALF:o + RW]),
                         (tile[lower, 4 * (XW + HALF) + t:4 * C:4], land[p, o:o + XW]))
                for a, b in parts:
                    if s == 0:
                        g.vector.tensor_copy(a, b).then_inc(cp, 1)
                    else:
                        g.scalar.activation(a, b, ActivationFunctionType.Copy).then_inc(cp, 1)
        g.vector.wait_ge(S["zt%d" % k], 2)
        g.vector.wait_ge(cp, 12)
        g.vector.quantize_mx(T["cq%d" % k][:], T["sq%d" % k][:], tile[:]).then_inc(S["qq%d" % k], 1)

    steps = [("cin0", "sin0", "arr0", arrivals(0)), ("cin1", "sin1", "arr1", arrivals(1)), ("cq3", "sq3", "qq3", 1),
             ("cin2", "sin2", "arr2", arrivals(2))]
    for j, (c, s, sem, n) in enumerate(steps):
        g.tensor.wait_ge(S[sem], n)
        for h, a in ((0, 0), (1, C - XW)):
            op = g.tensor.matmul_mx(T.ps[:, 512 * h:512 * h + HALF], T[c][:, a:a + XW], T[s][:, a:a + XW],
                                    T[c][:, XW:XW + HALF], T[s][:, XW:XW + HALF], j == 0, j == len(steps) - 1)
            if j == len(steps) - 1:
                op.then_inc(S["mm%d" % h], 1)

    g.vector.wait_ge(S["mm0"], 1)
    g.vector.tensor_copy(T.yo0[:], T.ps[:, 0:HALF]).then_inc(S["yc0"], 1)
    g.sync.wait_ge(S["yc0"], 1)
    g.sync.dma_start(T.y[:, 0:HALF], T.yo0[:]).then_inc(S["st0"], 16)
    g.sync.wait_ge(S["st0"], 16)
    g.scalar.wait_ge(S["mm1"], 1)
    g.scalar.activation(T.yo1[:], T.ps[:, 512:512 + HALF], ActivationFunctionType.Copy).then_inc(S["yc1"], 1)
    g.scalar.wait_ge(S["yc1"], 1)
    g.scalar.dma_start(T.y[:, HALF:GW], T.yo1[:]).then_inc(S["st1"], 16)
    g.scalar.wait_ge(S["st1"], 16)
